import numpy as np, ml_dtypes
CORES = [51,54,179,182]
N = 4
import mx_ref
BF = ml_dtypes.bfloat16
def entries(a):
    return np.ascontiguousarray(a.T).reshape(-1)
def table(e):
    return np.ascontiguousarray(np.reshape(e, (-1, 16)).T).astype(np.int32)
def f(rng, *shape):
    return mx_ref.flush((rng.standard_normal(shape, dtype=np.float32) * np.exp2(rng.integers(-2, 3, shape[:-1] + (1,)))).astype(BF))
def wide(rng, *shape, cols=0):
    v = rng.standard_normal(shape, dtype=np.float32) * np.exp2(rng.integers(-12, 13, shape)).astype(np.float32)
    if cols: v *= np.repeat(np.exp2(rng.integers(-cols, cols + 1, shape[:-2] + (1, shape[-1] // 4))) * (rng.random(shape[:-2] + (1, shape[-1] // 4)) > 0.0625), 4, axis=-1).astype(np.float32)
    return mx_ref.flush(v.astype(BF))
SH, CH, RD = 128, 64, 4
def lists(rng, same=False, apart=False, ends=False):
    a = []
    for r in range(N):
        p = rng.permutation(SH); e = []
        for t in range(1, RD):
            if same: c = p[:CH]
            elif apart: c = p[np.arange(CH * (t - 1), CH * t) % SH]
            elif ends: c = np.concatenate([[0, SH - 1], 1 + rng.permutation(SH - 2)[:CH - 2]])
            else: c = rng.permutation(SH)[:CH]
            e.append(rng.permutation(c))
        a.append(table(np.concatenate(e)))
    return {"idx": np.stack(a)}
def setup_inputs(rng):
    return {"wm": f(rng, N, 128, 4 * SH), "dl": f(rng, N, 128, (RD - 1) * 4 * CH), **lists(rng), "x": f(rng, N, 128, RD * 512)}
def setup_inputs_same(rng):
    return {**setup_inputs(rng), **lists(rng, same=True)}
def setup_inputs_apart(rng):
    return {**setup_inputs(rng), **lists(rng, apart=True)}
def setup_inputs_ends(rng):
    return {**setup_inputs(rng), **lists(rng, ends=True)}
def setup_inputs_big(rng):
    d = setup_inputs(rng); d["dl"] = (d["dl"].astype(np.float32) * np.float32(256)).astype(BF); return d
def setup_inputs_spread(rng):
    d = setup_inputs(rng); d["wm"] = wide(rng, N, 128, 4 * SH, cols=8); d["dl"] = wide(rng, N, 128, (RD - 1) * 4 * CH, cols=8); return d
def check_inputs(d):
    b = []
    for r in range(N):
        e = entries(d["idx"][r])
        if e.min() < 0 or e.max() >= SH: b.append("idx: range")
        for t in range(1, RD):
            if len(set(e[CH * (t - 1):CH * t].tolist())) != CH: b.append("idx: a column twice in one round")
    return b
def reference(wm, dl, idx, x):
    W = []
    for q in range(N):
        m = wm[q].reshape(128, SH, 4).copy(); d = dl[q].reshape(128, (RD - 1) * CH, 4); e = entries(idx[q])
        W.append([mx_ref.quantize(wm[q])])
        for t in range(1, RD):
            s = slice(CH * (t - 1), CH * t)
            m[:, e[s]] = (m[:, e[s]].astype(np.float32) + np.float32(0.25) * d[:, s].astype(np.float32)).astype(BF)
            W[q].append(mx_ref.quantize(m.reshape(128, 4 * SH).copy()))
    y = np.zeros((N, 128, RD * N * SH), np.float32)
    for r in range(N):
        for t in range(RD):
            X = mx_ref.quantize(np.ascontiguousarray(x[r][:, 512 * t:512 * t + 512]))
            for q in range(N):
                k = t * N + q
                y[r][:, SH * k:SH * k + SH] = mx_ref.matmul(X, W[q][t])
    return {"y": y}

@@ -1,0 +1,321 @@
+from concourse.bass import DstId, RemoteDMATransfer
+from concourse.mybir import dt, AluOpType, AxisListType, ActivationFunctionType
+
+SCRATCH = {
+    "m": ("sbuf", [128, 1280], "bfloat16"),
+    "dlb": ("sbuf", [128, 768], "bfloat16"),
+    "dq": ("sbuf", [128, 768], "bfloat16"),
+    "ltab": ("sbuf", [128, 12], "int32"),
+    "lrow": ("sbuf", [1, 192], "int32"),
+    "lb": ("sbuf", [128, 192], "int32"),
+    "pc": ("sbuf", [128, 192], "float32"),
+    "pcs": ("sbuf", [128, 192], "float32"),
+    "kk": ("sbuf", [128, 192], "float32"),
+    "v2": ("sbuf", [128, 256], "float32"),
+    "v3": ("sbuf", [128, 512], "float32"),
+    "vs": ("sbuf", [128, 192], "float32"),
+    "bi2": ("sbuf", [128, 4], "float32"),
+    "bi3": ("sbuf", [128, 4], "float32"),
+    "ba2": ("sbuf", [128, 4], "float32"),
+    "ba3": ("sbuf", [128, 4], "float32"),
+    "mn2": ("sbuf", [128, 4], "float32"),
+    "mn3": ("sbuf", [128, 4], "float32"),
+    "mm2": ("sbuf", [128, 4], "float32"),
+    "mm3": ("sbuf", [128, 4], "float32"),
+    "o1": ("sbuf", [128, 4], "uint16"),
+    "o2": ("sbuf", [128, 4], "uint16"),
+    "o3": ("sbuf", [128, 4], "uint16"),
+    "pi": ("sbuf", [128, 1], "int32"),
+    "pa": ("sbuf", [128, 1], "int32"),
+    "pb": ("sbuf", [128, 1], "int32"),
+    "pf": ("sbuf", [128, 1], "float32"),
+    "pj": ("sbuf", [128, 1], "float32"),
+    "bis": ("sbuf", [128, 1], "float32"),
+    "bas": ("sbuf", [128, 1], "float32"),
+    "mns": ("sbuf", [128, 3], "float32"),
+    "sown": ("sbuf", [128, 3], "uint16"),
+    "lst": ("sbuf", [128, 12], "uint16"),
+    "tab": ("sbuf", [128, 96], "uint16"),
+    "tabt": ("sbuf", [128, 96], "uint16"),
+    "cb": ("sbuf", [128, 512], "float8_e4m3fn_x4"),
+    "sb": ("sbuf", [128, 512], "uint8"),
+    "cd": ("sbuf", [128, 768], "float8_e4m3fn_x4"),
+    "sd": ("sbuf", [128, 768], "uint8"),
+    "xb": ("sbuf", [128, 2048], "bfloat16"),
+    "xq": ("sbuf", [128, 512], "float8_e4m3fn_x4"),
+    "xs": ("sbuf", [128, 512], "uint8"),
+    "yb": ("sbuf", [128, 2048], "float32"),
+    "ps": ("psum", [128, 4096], "float32"),
+}
+for _t in (1, 2, 3):
+    for _p in (0, 1):
+        SCRATCH["w%d%d" % (_t, _p)] = ("sbuf", [128, 640], "float32")
+
+SEMAPHORES = (["base%d" % q for q in range(4)] + ["chg%d" % q for q in range(4)] + ["lst%d" % q for q in range(4)]
+              + ["sent", "ldw", "ldt", "ldr", "ldd", "ldx", "iot", "bc", "fill", "pcs", "pab", "pf", "pj", "bis",
+                 "tb1", "tb2", "tb3", "dq1", "dq2", "dq3", "qb", "qd", "qx", "kk", "mn2", "mm2", "o2",
+                 "mn3", "mm3", "o3", "g1", "g2", "g3", "vs", "mns", "own", "ownd", "rep", "tabt", "st"]
+              + ["va%d" % s for s in range(4)] + ["vb%d" % s for s in range(4)]
+              + ["pb%d" % t for t in range(4)] + ["cb%d" % t for t in range(4)]
+              + ["pd%d%d" % (t, p) for t in (1, 2, 3) for p in (0, 1)]
+              + ["cd%d%d" % (t, p) for t in (1, 2, 3) for p in (0, 1)]
+              + ["ga%d%d" % (t, p) for t in (1, 2, 3) for p in (0, 1)])
+
+OP = AluOpType
+AF = ActivationFunctionType
+SH, CH, RD = 128, 64, 4
+
+
+def rank_program(g, core, T, topo):
+    rank = T.rank_of(core)
+    if rank is None:
+        return
+    S = T.sem
+    V, A, PE, SY = g.vector, g.scalar, g.tensor, g.sync
+    peers = [c for c in T.cores if c != core]
+    near = [c for c in peers if c in topo.cores_of(core)]
+    far = [c for c in peers if c not in topo.cores_of(core)]
+    near_r = [T.rank_of(c) for c in near]
+    far_r = [T.rank_of(c) for c in far]
+    far_e = topo.engines(core, far[0])
+    near_e = [e for e in topo.engines(core, near[0]) if e not in far_e]
+    half = rank % 2
+    mine, other = rank // 2, 1 - rank // 2
+
+    def ids(cores):
+        out = []
+        for c in cores:
+            rid, pid = topo.addr(c, core)
+            out.append(DstId(rid=rid, pnc=pid))
+        return out
+
+    def bits(engs):
+        return sum(1 << e for e in engs)
+
+    def send(dst, src, sem):
+        g.remote_dma_fused([
+            RemoteDMATransfer(dst_ids=ids(far), dma_engine_mask=bits(far_e), remote_sem=S[sem], srcs=[src], dsts=[dst] * len(far)),
+            RemoteDMATransfer(dst_ids=ids(near), dma_engine_mask=bits(near_e), remote_sem=S[sem], srcs=[src], dsts=[dst] * len(near)),
+        ], local_sem=S["sent"])
+        return len(far_e) + len(near_e)
+
+    nb = {}
+    for q in far_r:
+        nb[q] = len(far_e)
+    for q in near_r:
+        nb[q] = len(near_e)
+    cbv, sbv = T.cb[:, SH * rank:SH * rank + SH], T.sb[:, SH * rank:SH * rank + SH]
+    cdv, sdv = T.cd[:, 192 * rank:192 * rank + 192], T.sd[:, 192 * rank:192 * rank + 192]
+
+    SY.dma_start(T.m[:, 768:1280], T.wm[:]).then_inc(S["ldw"], 16)
+    for t in (1, 2, 3):
+        A.dma_start(T.lrow[0:1, CH * (t - 1):CH * t], T.idx[:, 4 * (t - 1):4 * t]).then_inc(S["ldr"], 16)
+    for k in range(4):
+        SY.dma_start(T.ltab[16 * k:16 * k + 16, :], T.idx[:]).then_inc(S["ldt"], 16)
+    A.dma_start(T.dlb[:], T.dl[:]).then_inc(S["ldd"], 16)
+    for k in range(4, 8):
+        A.dma_start(T.ltab[16 * k:16 * k + 16, :], T.idx[:]).then_inc(S["ldt"], 16)
+    SY.dma_start(T.xb[:], T.x[:]).then_inc(S["ldx"], 16)
+
+    g.iota(T.pi[:], [[0, 1]], 0, 1).then_inc(S["iot"], 1)
+    g.iota(T.pc[:], [[-CH, 3], [-0 + 1, 16], [16, 4]], 128, 0, allow_small_or_imprecise_dtypes=True).then_inc(S["iot"], 1)
+    g.wait_ge(S["ldr"], 48)
+    g.partition_broadcast(T.lb[:], T.lrow[0:1, :], 128).then_inc(S["bc"], 1)
+    sent = 0
+    g.wait_ge(S["qb"], 1)
+    sent += send(cbv.bitcast(dt.uint8), cbv.bitcast(dt.uint8), "base%d" % rank)
+    sent += send(sbv, sbv, "base%d" % rank)
+    g.wait_ge(S["own"], 1)
+    sent += send(T.lst[:, 3 * rank:3 * rank + 3], T.sown[:], "lst%d" % rank)
+    g.wait_ge(S["qd"], 1)
+    sent += send(cdv.bitcast(dt.uint8), cdv.bitcast(dt.uint8), "chg%d" % rank)
+    sent += send(sdv, sdv, "chg%d" % rank)
+    g.wait_ge(S["sent"], sent)
+
+    nf = 0
+    for t, w in ((1, 128), (2, 64)):
+        for p in (0, 1):
+            for h in (0, 192):
+                V.memset(T["w%d%d" % (t, p)][:, h:h + w], 0.0).then_inc(S["fill"], 1)
+                nf += 1
+    V.wait_ge(S["iot"], 2)
+    V.tensor_scalar(T.pcs[:], T.pc[:], 1.0 / 4096, None, OP.mult).then_inc(S["pcs"], 1)
+    V.tensor_scalar(T.pa[:], T.pi[:], 7, None, OP.bitwise_and).then_inc(S["pab"], 1)
+    V.tensor_scalar(T.pb[:], T.pi[:], 3, None, OP.logical_shift_right).then_inc(S["pab"], 1)
+    V.wait_ge(S["pab"], 2)
+    V.tensor_scalar(T.pf[:], T.pa[:], 16.0, None, OP.mult).then_inc(S["pf"], 1)
+    V.wait_ge(S["pf"], 1)
+    V.tensor_tensor(T.pj[:], T.pf[:], T.pb[:], OP.add).then_inc(S["pj"], 1)
+    V.wait_ge(S["pj"], 1)
+    V.tensor_scalar(T.bis[:], T.pj[:], -4096.0, float(192 * half), OP.mult, OP.add).then_inc(S["bis"], 1)
+    V.tensor_scalar(T.bas[:], T.pj[:], float(384 + SH * half), None, OP.add).then_inc(S["bis"], 1)
+    V.wait_ge(S["bis"], 2)
+    V.wait_ge(S["fill"], nf)
+    V.wait_ge(S["pcs"], 1)
+    V.wait_ge(S["ldw"], 16)
+    V.quantize_mx(cbv, sbv, T.m[:, 768:1280]).then_inc(S["qb"], 1)
+    V.wait_ge(S["ldt"], 128)
+    V.tensor_scalar(T.o1[:], T.ltab[:, 0:4], 4.0, None, OP.mult).then_inc(S["tb1"], 1)
+    V.tensor_scalar(T.bi2[:], T.ltab[:, 4:8], -16384.0, -512.0, OP.mult, OP.add).then_inc(S["tb2"], 1)
+    V.tensor_scalar(T.ba2[:], T.ltab[:, 4:8], 4.0, 256.0, OP.mult, OP.add).then_inc(S["tb2"], 1)
+    V.tensor_scalar(T.bi3[:], T.ltab[:, 8:12], -16384.0, -256.0, OP.mult, OP.add).then_inc(S["tb3"], 1)
+    V.tensor_scalar(T.ba3[:], T.ltab[:, 8:12], 4.0, 512.0, OP.mult, OP.add).then_inc(S["tb3"], 1)
+
+    def make(t, off):
+        lo = 256 * (RD - t)
+        for e in range(4):
+            V.tensor_tensor(T.m[:, lo - 256 + e:lo:4], T.m[:, lo + e:1280].indirect(off[:, 0:4]),
+                            T.dq[:, 256 * (t - 1) + e:256 * t:4], OP.add).then_inc(S["g%d" % t], 1)
+
+    V.wait_ge(S["dq1"], 1)
+    V.wait_ge(S["tb1"], 1)
+    make(1, T.o1)
+    V.wait_ge(S["bc"], 1)
+    V.tensor_tensor(T.kk[:], T.lb[:], T.pcs[:], OP.add).then_inc(S["kk"], 1)
+    for s in range(4):
+        V.wait_ge(S["va%d" % s], 1)
+        V.tensor_reduce(T.mn2[:, s:s + 1], T.v2[:, CH * s:CH * s + CH], AxisListType.X, OP.min).then_inc(S["mn2"], 1)
+    V.wait_ge(S["mn2"], 4)
+    V.wait_ge(S["tb2"], 2)
+    V.tensor_tensor(T.mm2[:], T.mn2[:], T.ba2[:], OP.min).then_inc(S["mm2"], 1)
+    V.wait_ge(S["mm2"], 1)
+    V.tensor_copy(T.o2[:], T.mm2[:]).then_inc(S["o2"], 1)
+    V.wait_ge(S["o2"], 1)
+    V.wait_ge(S["g1"], 4)
+    V.wait_ge(S["dq2"], 1)
+    make(2, T.o2)
+    V.wait_ge(S["vs"], 1)
+    for t in (1, 2, 3):
+        V.tensor_reduce(T.mns[:, t - 1:t], T.vs[:, 0:CH * t], AxisListType.X, OP.min).then_inc(S["mns"], 1)
+    for s in range(4):
+        V.wait_ge(S["vb%d" % s], 1)
+        V.tensor_reduce(T.mn3[:, s:s + 1], T.v3[:, 128 * s:128 * s + 128], AxisListType.X, OP.min).then_inc(S["mn3"], 1)
+        if s == 0:
+            V.wait_ge(S["mns"], 3)
+            V.tensor_scalar(T.sown[:], T.mns[:], T.bas[:], None, OP.min).then_inc(S["own"], 1)
+    V.wait_ge(S["mn3"], 4)
+    V.wait_ge(S["tb3"], 2)
+    V.tensor_tensor(T.mm3[:], T.mn3[:], T.ba3[:], OP.min).then_inc(S["mm3"], 1)
+    V.wait_ge(S["mm3"], 1)
+    V.tensor_copy(T.o3[:], T.mm3[:]).then_inc(S["o3"], 1)
+    V.wait_ge(S["o3"], 1)
+    V.wait_ge(S["g2"], 4)
+    V.wait_ge(S["dq3"], 1)
+    make(3, T.o3)
+    V.wait_ge(S["g3"], 4)
+    V.quantize_mx(cdv, sdv, T.m[:, 0:768]).then_inc(S["qd"], 1)
+    V.wait_ge(S["ldx"], 16)
+    V.quantize_mx(T.xq[:], T.xs[:], T.xb[:]).then_inc(S["qx"], 1)
+
+    A.wait_ge(S["ldd"], 16)
+    for t in (1, 2, 3):
+        A.activation(T.dq[:, 256 * (t - 1):256 * t], T.dlb[:, 256 * (t - 1):256 * t], AF.Copy, scale=0.25).then_inc(S["dq%d" % t], 1)
+    A.wait_ge(S["kk"], 1)
+    A.wait_ge(S["tb2"], 2)
+    for s in range(4):
+        A.activation(T.v2[:, CH * s:CH * s + CH], T.kk[:, 0:CH], AF.Abs, bias=T.bi2[:, s:s + 1], scale=16384.0).then_inc(S["va%d" % s], 1)
+    A.wait_ge(S["bis"], 2)
+    A.activation(T.vs[:], T.kk[:], AF.Abs, bias=T.bis[:], scale=4096.0).then_inc(S["vs"], 1)
+    A.wait_ge(S["tb3"], 2)
+    for s in range(4):
+        A.activation(T.v3[:, 128 * s:128 * s + 128], T.kk[:, 0:128], AF.Abs, bias=T.bi3[:, s:s + 1], scale=16384.0).then_inc(S["vb%d" % s], 1)
+
+    def bank(k, n):
+        return T.ps[:, 512 * k:512 * k + n]
+
+    def xt(t):
+        return T.xq[:, SH * t:SH * t + SH], T.xs[:, SH * t:SH * t + SH]
+
+    PE.wait_ge(S["qx"], 1)
+    PE.wait_ge(S["qb"], 1)
+    for q in near_r + far_r:
+        PE.wait_ge(S["base%d" % q], 2 * nb[q])
+    for t in range(RD):
+        PE.matmul_mx(bank(t, 512), xt(t)[0], xt(t)[1], T.cb[:], T.sb[:], True, True).then_inc(S["pb%d" % t], 1)
+    banks = {(1, mine): 4, (2, mine): 5, (3, mine): 6, (1, other): 7, (2, other): 0, (3, other): 1}
+
+    def changed(p):
+        for t in (1, 2, 3):
+            k = banks[(t, p)]
+            if k < RD:
+                PE.wait_ge(S["cb%d" % k], 1 if k == 0 else 2)
+            lo, hi = 384 * p + CH * (3 - t), 384 * p + 384
+            PE.matmul_mx(bank(k, hi - lo), xt(t)[0], xt(t)[1], T.cd[:, lo:hi], T.sd[:, lo:hi], True, True).then_inc(S["pd%d%d" % (t, p)], 1)
+
+    PE.wait_ge(S["qd"], 1)
+    for q in near_r:
+        PE.wait_ge(S["chg%d" % q], 2 * nb[q])
+    changed(mine)
+    for q in far_r:
+        PE.wait_ge(S["chg%d" % q], 2 * nb[q])
+    changed(other)
+
+    def vcopy(out, in_):
+        return V.tensor_copy(out, in_)
+
+    def acopy(out, in_):
+        return A.activation(out, in_, AF.Copy)
+
+    def base_copy(q, cp, t):
+        q.wait_ge(S["pb%d" % t], 1)
+        if t == 0:
+            cp(T.yb[:, 0:512], bank(0, 512)).then_inc(S["cb0"], 1)
+            return
+        for p in (0, 1):
+            cp(T["w%d%d" % (t, p)][:, 384:640], T.ps[:, 512 * t + 256 * p:512 * t + 256 * p + 256]).then_inc(S["cb%d" % t], 1)
+
+    def changed_copy(q, cp, t, p):
+        q.wait_ge(S["pd%d%d" % (t, p)], 1)
+        k, w = 512 * banks[(t, p)], T["w%d%d" % (t, p)]
+        if t == 3:
+            cp(w[:, 0:384], T.ps[:, k:k + 384]).then_inc(S["cd%d%d" % (t, p)], 1)
+            return
+        n = CH * t
+        for h in (0, 192):
+            cp(w[:, h + 192 - n:h + 192], T.ps[:, k + h:k + h + n]).then_inc(S["cd%d%d" % (t, p)], 1)
+
+    def pick(q, cp, t, p):
+        q.wait_ge(S["cb%d" % t], 2)
+        q.wait_ge(S["cd%d%d" % (t, p)], 1 if t == 3 else 2)
+        k = 8 * (4 * (t - 1) + 2 * p)
+        cp(T.yb[:, 512 * t + 256 * p:512 * t + 256 * p + 256], T["w%d%d" % (t, p)][:].indirect(T.tabt[:, k:k + 16])).then_inc(S["ga%d%d" % (t, p)], 1)
+
+    base_copy(A, acopy, 0)
+    A.wait_ge(S["cb0"], 1)
+    A.dma_start(T.y[:, 0:512], T.yb[:, 0:512]).then_inc(S["st"], 16)
+    base_copy(V, vcopy, 1)
+    base_copy(A, acopy, 2)
+    base_copy(V, vcopy, 3)
+    changed_copy(A, acopy, 1, mine)
+    changed_copy(A, acopy, 2, mine)
+    changed_copy(V, vcopy, 3, mine)
+    V.wait_ge(S["rep"], 128)
+    for t in (1, 2, 3):
+        for q in range(4):
+            k = 8 * (4 * (t - 1) + q)
+            V.tensor_copy(T.tabt[:, k:k + 8], T.tab[:, 3 * q + t - 1:96:12]).then_inc(S["tabt"], 1)
+    A.wait_ge(S["tabt"], 12)
+    V.wait_ge(S["tabt"], 12)
+    pick(A, acopy, 1, mine)
+    pick(V, vcopy, 3, mine)
+    pick(A, acopy, 2, mine)
+    changed_copy(A, acopy, 1, other)
+    changed_copy(V, vcopy, 2, other)
+    pick(A, acopy, 1, other)
+    changed_copy(V, vcopy, 3, other)
+    pick(A, acopy, 2, other)
+    pick(V, vcopy, 3, other)
+
+    SY.wait_ge(S["own"], 1)
+    SY.dma_start(T.lst[:, 3 * rank:3 * rank + 3], T.sown[:]).then_inc(S["ownd"], 16)
+    SY.wait_ge(S["ownd"], 16)
+    for q in near_r + far_r:
+        SY.wait_ge(S["lst%d" % q], nb[q])
+    for k in range(8):
+        SY.dma_start(T.tab[16 * k:16 * k + 16, :], T.lst[:]).then_inc(S["rep"], 16)
+    for p, order in ((mine, (1, 3, 2)), (other, (1, 2, 3))):
+        for t in order:
+            SY.wait_ge(S["ga%d%d" % (t, p)], 1)
+            c = 512 * t + 256 * p
+            SY.dma_start(T.y[:, c:c + 256], T.yb[:, c:c + 256]).then_inc(S["st"], 16)
+    SY.wait_ge(S["st"], 16 * 7)

@@ -11,17 +11,13 @@ SCRATCH = {
     "pc": ("sbuf", [128, 192], "float32"),
     "pcs": ("sbuf", [128, 192], "float32"),
     "kk": ("sbuf", [128, 192], "float32"),
-    "v2": ("sbuf", [128, 256], "float32"),
-    "v3": ("sbuf", [128, 512], "float32"),
+    "v2": ("sbuf", [128, 260], "float32"),
+    "v3": ("sbuf", [128, 516], "float32"),
     "vs": ("sbuf", [128, 192], "float32"),
-    "bi2": ("sbuf", [128, 4], "float32"),
-    "bi3": ("sbuf", [128, 4], "float32"),
-    "ba2": ("sbuf", [128, 4], "float32"),
-    "ba3": ("sbuf", [128, 4], "float32"),
+    "vm": ("sbuf", [128, 192], "float32"),
+    "bi": ("sbuf", [128, 8], "float32"),
     "mn2": ("sbuf", [128, 4], "float32"),
     "mn3": ("sbuf", [128, 4], "float32"),
-    "mm2": ("sbuf", [128, 4], "float32"),
-    "mm3": ("sbuf", [128, 4], "float32"),
     "o1": ("sbuf", [128, 4], "uint16"),
     "o2": ("sbuf", [128, 4], "uint16"),
     "o3": ("sbuf", [128, 4], "uint16"),
@@ -32,7 +28,6 @@ SCRATCH = {
     "pj": ("sbuf", [128, 1], "float32"),
     "bis": ("sbuf", [128, 1], "float32"),
     "bas": ("sbuf", [128, 1], "float32"),
-    "mns": ("sbuf", [128, 3], "float32"),
     "sown": ("sbuf", [128, 3], "uint16"),
     "lst": ("sbuf", [128, 12], "uint16"),
     "tab": ("sbuf", [128, 96], "uint16"),
@@ -52,14 +47,12 @@ for _t in (1, 2, 3):
         SCRATCH["w%d%d" % (_t, _p)] = ("sbuf", [128, 640], "float32")
 
 SEMAPHORES = (["base%d" % q for q in range(4)] + ["chg%d" % q for q in range(4)] + ["lst%d" % q for q in range(4)]
-              + ["sent", "ldw", "ldt", "ldr", "ldd", "ldx", "iot", "bc", "fill", "pcs", "pab", "pf", "pj", "bis",
-                 "tb1", "tb2", "tb3", "dq1", "dq2", "dq3", "qb", "qd", "qx", "kk", "mn2", "mm2", "o2",
-                 "mn3", "mm3", "o3", "g1", "g2", "g3", "vs", "mns", "own", "ownd", "rep", "tabt", "st"]
+              + ["sent", "ldw", "ldt", "ldr1", "ldr", "ldd", "ldx", "iot", "bc1", "bc2", "fill", "pcs", "pab", "pf", "pj", "bis",
+                 "tb1", "tb2", "ba", "dq1", "dq2", "dq3", "qb", "qd", "qx", "kk1", "kk2", "mn2", "o2",
+                 "mn3", "o3", "g1", "g2", "g3", "vs", "vm", "own", "ownd", "rep", "st"]
               + ["va%d" % s for s in range(4)] + ["vb%d" % s for s in range(4)]
               + ["pb%d" % t for t in range(4)] + ["cb%d" % t for t in range(4)]
-              + ["pd%d%d" % (t, p) for t in (1, 2, 3) for p in (0, 1)]
-              + ["cd%d%d" % (t, p) for t in (1, 2, 3) for p in (0, 1)]
-              + ["ga%d%d" % (t, p) for t in (1, 2, 3) for p in (0, 1)])
+              + ["%s%d%d" % (n, t, p) for n in ("pd", "cd", "ga", "tt") for t in (1, 2, 3) for p in (0, 1)])
 
 OP = AluOpType
 AF = ActivationFunctionType
@@ -78,7 +71,7 @@ def rank_program(g, core, T, topo):
     near_r = [T.rank_of(c) for c in near]
     far_r = [T.rank_of(c) for c in far]
     far_e = topo.engines(core, far[0])
-    near_e = [e for e in topo.engines(core, near[0]) if e not in far_e]
+    near_e = [e for e in topo.engines(core, near[0]) if e not in far_e][:len(far_e) * len(near) // len(far)]
     half = rank % 2
     mine, other = rank // 2, 1 - rank // 2
 
@@ -107,43 +100,49 @@ def rank_program(g, core, T, topo):
     cbv, sbv = T.cb[:, SH * rank:SH * rank + SH], T.sb[:, SH * rank:SH * rank + SH]
     cdv, sdv = T.cd[:, 192 * rank:192 * rank + 192], T.sd[:, 192 * rank:192 * rank + 192]
 
+    def row(t):
+        A.dma_start(T.lrow[0:1, CH * (t - 1):CH * t], T.idx[:, 4 * (t - 1):4 * t]).then_inc(S["ldr1" if t == 1 else "ldr"], 16)
+
     SY.dma_start(T.m[:, 768:1280], T.wm[:]).then_inc(S["ldw"], 16)
-    for t in (1, 2, 3):
-        A.dma_start(T.lrow[0:1, CH * (t - 1):CH * t], T.idx[:, 4 * (t - 1):4 * t]).then_inc(S["ldr"], 16)
-    for k in range(4):
-        SY.dma_start(T.ltab[16 * k:16 * k + 16, :], T.idx[:]).then_inc(S["ldt"], 16)
+    row(1)
     A.dma_start(T.dlb[:], T.dl[:]).then_inc(S["ldd"], 16)
-    for k in range(4, 8):
+    row(2)
+    row(3)
+    for k in range(5):
+        SY.dma_start(T.ltab[16 * k:16 * k + 16, :], T.idx[:]).then_inc(S["ldt"], 16)
+    for k in range(5, 8):
         A.dma_start(T.ltab[16 * k:16 * k + 16, :], T.idx[:]).then_inc(S["ldt"], 16)
     SY.dma_start(T.xb[:], T.x[:]).then_inc(S["ldx"], 16)
 
     g.iota(T.pi[:], [[0, 1]], 0, 1).then_inc(S["iot"], 1)
-    g.iota(T.pc[:], [[-CH, 3], [-0 + 1, 16], [16, 4]], 128, 0, allow_small_or_imprecise_dtypes=True).then_inc(S["iot"], 1)
-    g.wait_ge(S["ldr"], 48)
-    g.partition_broadcast(T.lb[:], T.lrow[0:1, :], 128).then_inc(S["bc"], 1)
+    g.iota(T.pc[:], [[-CH, 3], [1, 16], [16, 4]], 128, 0, allow_small_or_imprecise_dtypes=True).then_inc(S["iot"], 1)
+    g.wait_ge(S["ldr1"], 16)
+    g.partition_broadcast(T.lb[:, 0:CH], T.lrow[0:1, 0:CH], 128).then_inc(S["bc1"], 1)
+    g.wait_ge(S["ldr"], 32)
+    g.partition_broadcast(T.lb[:, CH:192], T.lrow[0:1, CH:192], 128).then_inc(S["bc2"], 1)
     sent = 0
     g.wait_ge(S["qb"], 1)
     sent += send(cbv.bitcast(dt.uint8), cbv.bitcast(dt.uint8), "base%d" % rank)
-    sent += send(sbv, sbv, "base%d" % rank)
     g.wait_ge(S["own"], 1)
     sent += send(T.lst[:, 3 * rank:3 * rank + 3], T.sown[:], "lst%d" % rank)
+    sent += send(sbv, sbv, "base%d" % rank)
     g.wait_ge(S["qd"], 1)
     sent += send(cdv.bitcast(dt.uint8), cdv.bitcast(dt.uint8), "chg%d" % rank)
     sent += send(sdv, sdv, "chg%d" % rank)
     g.wait_ge(S["sent"], sent)
 
     nf = 0
-    for t, w in ((1, 128), (2, 64)):
-        for p in (0, 1):
-            for h in (0, 192):
-                V.memset(T["w%d%d" % (t, p)][:, h:h + w], 0.0).then_inc(S["fill"], 1)
-                nf += 1
     V.wait_ge(S["iot"], 2)
     V.tensor_scalar(T.pcs[:], T.pc[:], 1.0 / 4096, None, OP.mult).then_inc(S["pcs"], 1)
     V.tensor_scalar(T.pa[:], T.pi[:], 7, None, OP.bitwise_and).then_inc(S["pab"], 1)
     V.tensor_scalar(T.pb[:], T.pi[:], 3, None, OP.logical_shift_right).then_inc(S["pab"], 1)
     V.wait_ge(S["pab"], 2)
     V.tensor_scalar(T.pf[:], T.pa[:], 16.0, None, OP.mult).then_inc(S["pf"], 1)
+    for t, w in ((1, 128), (2, 64)):
+        for p in (0, 1):
+            for h in (0, 192):
+                V.memset(T["w%d%d" % (t, p)][:, h:h + w], 0.0).then_inc(S["fill"], 1)
+                nf += 1
     V.wait_ge(S["pf"], 1)
     V.tensor_tensor(T.pj[:], T.pf[:], T.pb[:], OP.add).then_inc(S["pj"], 1)
     V.wait_ge(S["pj"], 1)
@@ -155,11 +154,12 @@ def rank_program(g, core, T, topo):
     V.wait_ge(S["ldw"], 16)
     V.quantize_mx(cbv, sbv, T.m[:, 768:1280]).then_inc(S["qb"], 1)
     V.wait_ge(S["ldt"], 128)
+    V.tensor_scalar(T.bi[:], T.ltab[:, 4:12], -16384.0, -256.0, OP.mult, OP.add).then_inc(S["tb2"], 1)
     V.tensor_scalar(T.o1[:], T.ltab[:, 0:4], 4.0, None, OP.mult).then_inc(S["tb1"], 1)
-    V.tensor_scalar(T.bi2[:], T.ltab[:, 4:8], -16384.0, -512.0, OP.mult, OP.add).then_inc(S["tb2"], 1)
-    V.tensor_scalar(T.ba2[:], T.ltab[:, 4:8], 4.0, 256.0, OP.mult, OP.add).then_inc(S["tb2"], 1)
-    V.tensor_scalar(T.bi3[:], T.ltab[:, 8:12], -16384.0, -256.0, OP.mult, OP.add).then_inc(S["tb3"], 1)
-    V.tensor_scalar(T.ba3[:], T.ltab[:, 8:12], 4.0, 512.0, OP.mult, OP.add).then_inc(S["tb3"], 1)
+    V.tensor_scalar(T.v2[:, 64:260:65], T.ltab[:, 4:8], 4.0, 512.0, OP.mult, OP.add).then_inc(S["ba"], 1)
+    V.tensor_scalar(T.v3[:, 128:516:129], T.ltab[:, 8:12], 4.0, 512.0, OP.mult, OP.add).then_inc(S["ba"], 1)
+    V.wait_ge(S["bc1"], 1)
+    V.tensor_tensor(T.kk[:, 0:CH], T.lb[:, 0:CH], T.pcs[:, 0:CH], OP.add).then_inc(S["kk1"], 1)
 
     def make(t, off):
         lo = 256 * (RD - t)
@@ -167,37 +167,30 @@ def rank_program(g, core, T, topo):
             V.tensor_tensor(T.m[:, lo - 256 + e:lo:4], T.m[:, lo + e:1280].indirect(off[:, 0:4]),
                             T.dq[:, 256 * (t - 1) + e:256 * t:4], OP.add).then_inc(S["g%d" % t], 1)
 
-    V.wait_ge(S["dq1"], 1)
     V.wait_ge(S["tb1"], 1)
+    V.wait_ge(S["dq1"], 1)
     make(1, T.o1)
-    V.wait_ge(S["bc"], 1)
-    V.tensor_tensor(T.kk[:], T.lb[:], T.pcs[:], OP.add).then_inc(S["kk"], 1)
+    V.wait_ge(S["bc2"], 1)
+    V.tensor_tensor(T.kk[:, CH:192], T.lb[:, CH:192], T.pcs[:, CH:192], OP.add).then_inc(S["kk2"], 1)
+    V.wait_ge(S["ba"], 2)
     for s in range(4):
         V.wait_ge(S["va%d" % s], 1)
-        V.tensor_reduce(T.mn2[:, s:s + 1], T.v2[:, CH * s:CH * s + CH], AxisListType.X, OP.min).then_inc(S["mn2"], 1)
+        V.tensor_reduce(T.mn2[:, s:s + 1], T.v2[:, 65 * s:65 * s + 65], AxisListType.X, OP.min).then_inc(S["mn2"], 1)
+    V.wait_ge(S["vs"], 1)
+    V.tensor_tensor_scan(T.vm[:], T.vs[:], T.vs[:], 1.0e9, OP.min, OP.min).then_inc(S["vm"], 1)
     V.wait_ge(S["mn2"], 4)
-    V.wait_ge(S["tb2"], 2)
-    V.tensor_tensor(T.mm2[:], T.mn2[:], T.ba2[:], OP.min).then_inc(S["mm2"], 1)
-    V.wait_ge(S["mm2"], 1)
-    V.tensor_copy(T.o2[:], T.mm2[:]).then_inc(S["o2"], 1)
+    V.tensor_scalar(T.o2[:], T.mn2[:], -256.0, None, OP.add).then_inc(S["o2"], 1)
+    V.wait_ge(S["vm"], 1)
+    V.tensor_scalar(T.sown[:], T.vm[:, CH - 1:192:CH], T.bas[:], None, OP.min).then_inc(S["own"], 1)
     V.wait_ge(S["o2"], 1)
     V.wait_ge(S["g1"], 4)
     V.wait_ge(S["dq2"], 1)
     make(2, T.o2)
-    V.wait_ge(S["vs"], 1)
-    for t in (1, 2, 3):
-        V.tensor_reduce(T.mns[:, t - 1:t], T.vs[:, 0:CH * t], AxisListType.X, OP.min).then_inc(S["mns"], 1)
     for s in range(4):
         V.wait_ge(S["vb%d" % s], 1)
-        V.tensor_reduce(T.mn3[:, s:s + 1], T.v3[:, 128 * s:128 * s + 128], AxisListType.X, OP.min).then_inc(S["mn3"], 1)
-        if s == 0:
-            V.wait_ge(S["mns"], 3)
-            V.tensor_scalar(T.sown[:], T.mns[:], T.bas[:], None, OP.min).then_inc(S["own"], 1)
+        V.tensor_reduce(T.mn3[:, s:s + 1], T.v3[:, 129 * s:129 * s + 129], AxisListType.X, OP.min).then_inc(S["mn3"], 1)
     V.wait_ge(S["mn3"], 4)
-    V.wait_ge(S["tb3"], 2)
-    V.tensor_tensor(T.mm3[:], T.mn3[:], T.ba3[:], OP.min).then_inc(S["mm3"], 1)
-    V.wait_ge(S["mm3"], 1)
-    V.tensor_copy(T.o3[:], T.mm3[:]).then_inc(S["o3"], 1)
+    V.tensor_copy(T.o3[:], T.mn3[:]).then_inc(S["o3"], 1)
     V.wait_ge(S["o3"], 1)
     V.wait_ge(S["g2"], 4)
     V.wait_ge(S["dq3"], 1)
@@ -207,18 +200,22 @@ def rank_program(g, core, T, topo):
     V.wait_ge(S["ldx"], 16)
     V.quantize_mx(T.xq[:], T.xs[:], T.xb[:]).then_inc(S["qx"], 1)
 
-    A.wait_ge(S["ldd"], 16)
-    for t in (1, 2, 3):
+    def quarter(t):
         A.activation(T.dq[:, 256 * (t - 1):256 * t], T.dlb[:, 256 * (t - 1):256 * t], AF.Copy, scale=0.25).then_inc(S["dq%d" % t], 1)
-    A.wait_ge(S["kk"], 1)
-    A.wait_ge(S["tb2"], 2)
+
+    A.wait_ge(S["ldd"], 16)
+    quarter(1)
+    A.wait_ge(S["tb2"], 1)
+    A.wait_ge(S["kk1"], 1)
     for s in range(4):
-        A.activation(T.v2[:, CH * s:CH * s + CH], T.kk[:, 0:CH], AF.Abs, bias=T.bi2[:, s:s + 1], scale=16384.0).then_inc(S["va%d" % s], 1)
+        A.activation(T.v2[:, 65 * s:65 * s + CH], T.kk[:, 0:CH], AF.Abs, bias=T.bi[:, s:s + 1], scale=16384.0).then_inc(S["va%d" % s], 1)
+    quarter(2)
+    A.wait_ge(S["kk2"], 1)
     A.wait_ge(S["bis"], 2)
     A.activation(T.vs[:], T.kk[:], AF.Abs, bias=T.bis[:], scale=4096.0).then_inc(S["vs"], 1)
-    A.wait_ge(S["tb3"], 2)
     for s in range(4):
-        A.activation(T.v3[:, 128 * s:128 * s + 128], T.kk[:, 0:128], AF.Abs, bias=T.bi3[:, s:s + 1], scale=16384.0).then_inc(S["vb%d" % s], 1)
+        A.activation(T.v3[:, 129 * s:129 * s + 128], T.kk[:, 0:128], AF.Abs, bias=T.bi[:, 4 + s:5 + s], scale=16384.0).then_inc(S["vb%d" % s], 1)
+    quarter(3)
 
     def bank(k, n):
         return T.ps[:, 512 * k:512 * k + n]
@@ -274,11 +271,18 @@ def rank_program(g, core, T, topo):
         for h in (0, 192):
             cp(w[:, h + 192 - n:h + 192], T.ps[:, k + h:k + h + n]).then_inc(S["cd%d%d" % (t, p)], 1)
 
-    def pick(q, cp, t, p):
+    def order(t, p):
+        for h in (0, 1):
+            q = 2 * p + h
+            k = 8 * (4 * (t - 1) + q)
+            V.tensor_copy(T.tabt[:, k:k + 8], T.tab[:, 3 * q + t - 1:96:12]).then_inc(S["tt%d%d" % (t, p)], 1)
+
+    def pick(q, cp, t, p, lo=0, hi=2):
+        q.wait_ge(S["tt%d%d" % (t, p)], 2)
         q.wait_ge(S["cb%d" % t], 2)
         q.wait_ge(S["cd%d%d" % (t, p)], 1 if t == 3 else 2)
-        k = 8 * (4 * (t - 1) + 2 * p)
-        cp(T.yb[:, 512 * t + 256 * p:512 * t + 256 * p + 256], T["w%d%d" % (t, p)][:].indirect(T.tabt[:, k:k + 16])).then_inc(S["ga%d%d" % (t, p)], 1)
+        k, c = 8 * (4 * (t - 1) + 2 * p), 512 * t + 256 * p
+        cp(T.yb[:, c + SH * lo:c + SH * hi], T["w%d%d" % (t, p)][:].indirect(T.tabt[:, k + 8 * lo:k + 8 * hi])).then_inc(S["ga%d%d" % (t, p)], hi - lo)
 
     base_copy(A, acopy, 0)
     A.wait_ge(S["cb0"], 1)
@@ -290,21 +294,21 @@ def rank_program(g, core, T, topo):
     changed_copy(A, acopy, 2, mine)
     changed_copy(V, vcopy, 3, mine)
     V.wait_ge(S["rep"], 128)
-    for t in (1, 2, 3):
-        for q in range(4):
-            k = 8 * (4 * (t - 1) + q)
-            V.tensor_copy(T.tabt[:, k:k + 8], T.tab[:, 3 * q + t - 1:96:12]).then_inc(S["tabt"], 1)
-    A.wait_ge(S["tabt"], 12)
-    V.wait_ge(S["tabt"], 12)
+    order(1, mine)
+    order(2, mine)
+    order(3, mine)
     pick(A, acopy, 1, mine)
-    pick(V, vcopy, 3, mine)
     pick(A, acopy, 2, mine)
+    pick(V, vcopy, 3, mine)
+    for t in (1, 2, 3):
+        order(t, other)
     changed_copy(A, acopy, 1, other)
     changed_copy(V, vcopy, 2, other)
     pick(A, acopy, 1, other)
     changed_copy(V, vcopy, 3, other)
     pick(A, acopy, 2, other)
-    pick(V, vcopy, 3, other)
+    pick(V, vcopy, 3, other, 0, 1)
+    pick(A, acopy, 3, other, 1, 2)
 
     SY.wait_ge(S["own"], 1)
     SY.dma_start(T.lst[:, 3 * rank:3 * rank + 3], T.sown[:]).then_inc(S["ownd"], 16)
@@ -313,9 +317,9 @@ def rank_program(g, core, T, topo):
         SY.wait_ge(S["lst%d" % q], nb[q])
     for k in range(8):
         SY.dma_start(T.tab[16 * k:16 * k + 16, :], T.lst[:]).then_inc(S["rep"], 16)
-    for p, order in ((mine, (1, 3, 2)), (other, (1, 2, 3))):
-        for t in order:
-            SY.wait_ge(S["ga%d%d" % (t, p)], 1)
+    for p, turn in ((mine, (1, 3, 2)), (other, (1, 2, 3))):
+        for t in turn:
+            SY.wait_ge(S["ga%d%d" % (t, p)], 2)
             c = 512 * t + 256 * p
             SY.dma_start(T.y[:, c:c + 256], T.yb[:, c:c + 256]).then_inc(S["st"], 16)
     SY.wait_ge(S["st"], 16 * 7)

@@ -11,13 +11,15 @@ SCRATCH = {
     "pc": ("sbuf", [128, 192], "float32"),
     "pcs": ("sbuf", [128, 192], "float32"),
     "kk": ("sbuf", [128, 192], "float32"),
-    "v2": ("sbuf", [128, 260], "float32"),
-    "v3": ("sbuf", [128, 516], "float32"),
+    "v2": ("sbuf", [128, 260], "bfloat16"),
+    "v3": ("sbuf", [128, 516], "bfloat16"),
+    "r2": ("sbuf", [128, 260], "bfloat16"),
+    "r3": ("sbuf", [128, 516], "bfloat16"),
+    "s2": ("sbuf", [128, 260], "bfloat16"),
+    "s3": ("sbuf", [128, 516], "bfloat16"),
     "vs": ("sbuf", [128, 192], "float32"),
     "vm": ("sbuf", [128, 192], "float32"),
     "bi": ("sbuf", [128, 8], "float32"),
-    "mn2": ("sbuf", [128, 4], "float32"),
-    "mn3": ("sbuf", [128, 4], "float32"),
     "o1": ("sbuf", [128, 4], "uint16"),
     "o2": ("sbuf", [128, 4], "uint16"),
     "o3": ("sbuf", [128, 4], "uint16"),
@@ -46,17 +48,17 @@ for _t in (1, 2, 3):
     for _p in (0, 1):
         SCRATCH["w%d%d" % (_t, _p)] = ("sbuf", [128, 640], "float32")
 
-SEMAPHORES = (["base%d" % q for q in range(4)] + ["chg%d" % q for q in range(4)] + ["lst%d" % q for q in range(4)]
-              + ["sent", "ldw", "ldt", "ldr1", "ldr", "ldd", "ldx", "iot", "bc1", "bc2", "fill", "pcs", "pab", "pf", "pj", "bis",
-                 "tb1", "tb2", "ba", "dq1", "dq2", "dq3", "qb", "qd", "qx", "kk1", "kk2", "mn2", "o2",
-                 "mn3", "o3", "g1", "g2", "g3", "vs", "vm", "own", "ownd", "rep", "st"]
-              + ["va%d" % s for s in range(4)] + ["vb%d" % s for s in range(4)]
-              + ["pb%d" % t for t in range(4)] + ["cb%d" % t for t in range(4)]
+SEMAPHORES = (["%s%d" % (n, q) for n in ("base", "chg", "lst") for q in range(4)]
+              + ["sent", "ldw", "ldt", "ldr1", "ldr", "ldd", "ldx", "iot", "bc1", "bc2", "fill", "rz", "rs", "pcs", "pab", "pf",
+                 "pj", "bis", "tb1", "tb2", "ba", "dq1", "dq2", "dq3", "qb", "qd", "kk1", "kk2", "va", "vb", "s2", "o2",
+                 "s3", "o3", "g1", "g2", "g3", "vs", "vm", "own", "ownd", "rep", "st"]
+              + ["%s%d" % (n, t) for n in ("qx", "pb", "cb") for t in range(4)]
               + ["%s%d%d" % (n, t, p) for n in ("pd", "cd", "ga", "tt") for t in (1, 2, 3) for p in (0, 1)])
 
 OP = AluOpType
 AF = ActivationFunctionType
 SH, CH, RD = 128, 64, 4
+LARGE = 2.0 ** 20
 
 
 def rank_program(g, core, T, topo):
@@ -131,74 +133,78 @@ def rank_program(g, core, T, topo):
     sent += send(sdv, sdv, "chg%d" % rank)
     g.wait_ge(S["sent"], sent)
 
-    nf = 0
+    V.memset(T.r2[:], 0.0).then_inc(S["rz"], 1)
+    V.memset(T.r3[:], 0.0).then_inc(S["rz"], 1)
+    V.memset(T.w10[:, 192:320], 0.0).then_inc(S["fill"], 1)
+    V.memset(T.w11[:, 192:320], 0.0).then_inc(S["fill"], 1)
     V.wait_ge(S["iot"], 2)
     V.tensor_scalar(T.pcs[:], T.pc[:], 1.0 / 4096, None, OP.mult).then_inc(S["pcs"], 1)
     V.tensor_scalar(T.pa[:], T.pi[:], 7, None, OP.bitwise_and).then_inc(S["pab"], 1)
     V.tensor_scalar(T.pb[:], T.pi[:], 3, None, OP.logical_shift_right).then_inc(S["pab"], 1)
+    V.wait_ge(S["rz"], 2)
+    V.memset(T.r2[:, 0:260:65], LARGE).then_inc(S["rs"], 1)
+    V.memset(T.r3[:, 0:516:129], LARGE).then_inc(S["rs"], 1)
     V.wait_ge(S["pab"], 2)
     V.tensor_scalar(T.pf[:], T.pa[:], 16.0, None, OP.mult).then_inc(S["pf"], 1)
-    for t, w in ((1, 128), (2, 64)):
-        for p in (0, 1):
-            for h in (0, 192):
-                V.memset(T["w%d%d" % (t, p)][:, h:h + w], 0.0).then_inc(S["fill"], 1)
-                nf += 1
     V.wait_ge(S["pf"], 1)
     V.tensor_tensor(T.pj[:], T.pf[:], T.pb[:], OP.add).then_inc(S["pj"], 1)
     V.wait_ge(S["pj"], 1)
     V.tensor_scalar(T.bis[:], T.pj[:], -4096.0, float(192 * half), OP.mult, OP.add).then_inc(S["bis"], 1)
     V.tensor_scalar(T.bas[:], T.pj[:], float(384 + SH * half), None, OP.add).then_inc(S["bis"], 1)
     V.wait_ge(S["bis"], 2)
-    V.wait_ge(S["fill"], nf)
+    V.wait_ge(S["rs"], 2)
+    V.wait_ge(S["fill"], 2)
     V.wait_ge(S["pcs"], 1)
     V.wait_ge(S["ldw"], 16)
     V.quantize_mx(cbv, sbv, T.m[:, 768:1280]).then_inc(S["qb"], 1)
     V.wait_ge(S["ldt"], 128)
-    V.tensor_scalar(T.bi[:], T.ltab[:, 4:12], -16384.0, -256.0, OP.mult, OP.add).then_inc(S["tb2"], 1)
+    V.tensor_scalar(T.bi[:], T.ltab[:, 4:12], -4096.0, -64.0, OP.mult, OP.add).then_inc(S["tb2"], 1)
     V.tensor_scalar(T.o1[:], T.ltab[:, 0:4], 4.0, None, OP.mult).then_inc(S["tb1"], 1)
-    V.tensor_scalar(T.v2[:, 64:260:65], T.ltab[:, 4:8], 4.0, 512.0, OP.mult, OP.add).then_inc(S["ba"], 1)
-    V.tensor_scalar(T.v3[:, 128:516:129], T.ltab[:, 8:12], 4.0, 512.0, OP.mult, OP.add).then_inc(S["ba"], 1)
+    V.tensor_scalar(T.v2[:, 64:260:65], T.ltab[:, 4:8], 128.0, None, OP.add).then_inc(S["ba"], 1)
+    V.tensor_scalar(T.v3[:, 128:516:129], T.ltab[:, 8:12], 128.0, None, OP.add).then_inc(S["ba"], 1)
     V.wait_ge(S["bc1"], 1)
     V.tensor_tensor(T.kk[:, 0:CH], T.lb[:, 0:CH], T.pcs[:, 0:CH], OP.add).then_inc(S["kk1"], 1)
 
-    def make(t, off):
+    def make(t, off, *es):
         lo = 256 * (RD - t)
-        for e in range(4):
+        for e in es:
             V.tensor_tensor(T.m[:, lo - 256 + e:lo:4], T.m[:, lo + e:1280].indirect(off[:, 0:4]),
                             T.dq[:, 256 * (t - 1) + e:256 * t:4], OP.add).then_inc(S["g%d" % t], 1)
 
     V.wait_ge(S["tb1"], 1)
     V.wait_ge(S["dq1"], 1)
-    make(1, T.o1)
+    make(1, T.o1, 0, 1, 2)
     V.wait_ge(S["bc2"], 1)
     V.tensor_tensor(T.kk[:, CH:192], T.lb[:, CH:192], T.pcs[:, CH:192], OP.add).then_inc(S["kk2"], 1)
     V.wait_ge(S["ba"], 2)
-    for s in range(4):
-        V.wait_ge(S["va%d" % s], 1)
-        V.tensor_reduce(T.mn2[:, s:s + 1], T.v2[:, 65 * s:65 * s + 65], AxisListType.X, OP.min).then_inc(S["mn2"], 1)
+    V.wait_ge(S["va"], 4)
+    V.tensor_tensor_scan(T.s2[:], T.r2[:], T.v2[:], 2 * LARGE, OP.add, OP.min).then_inc(S["s2"], 1)
+    make(1, T.o1, 3)
+    V.wait_ge(S["s2"], 1)
+    V.tensor_scalar(T.o2[:], T.s2[:, 64:260:65], 4.0, -256.0, OP.mult, OP.add).then_inc(S["o2"], 1)
     V.wait_ge(S["vs"], 1)
     V.tensor_tensor_scan(T.vm[:], T.vs[:], T.vs[:], 1.0e9, OP.min, OP.min).then_inc(S["vm"], 1)
-    V.wait_ge(S["mn2"], 4)
-    V.tensor_scalar(T.o2[:], T.mn2[:], -256.0, None, OP.add).then_inc(S["o2"], 1)
-    V.wait_ge(S["vm"], 1)
-    V.tensor_scalar(T.sown[:], T.vm[:, CH - 1:192:CH], T.bas[:], None, OP.min).then_inc(S["own"], 1)
     V.wait_ge(S["o2"], 1)
     V.wait_ge(S["g1"], 4)
     V.wait_ge(S["dq2"], 1)
-    make(2, T.o2)
-    for s in range(4):
-        V.wait_ge(S["vb%d" % s], 1)
-        V.tensor_reduce(T.mn3[:, s:s + 1], T.v3[:, 129 * s:129 * s + 129], AxisListType.X, OP.min).then_inc(S["mn3"], 1)
-    V.wait_ge(S["mn3"], 4)
-    V.tensor_copy(T.o3[:], T.mn3[:]).then_inc(S["o3"], 1)
+    V.wait_ge(S["vm"], 1)
+    V.tensor_scalar(T.sown[:], T.vm[:, CH - 1:192:CH], T.bas[:], None, OP.min).then_inc(S["own"], 1)
+    make(2, T.o2, 0, 1)
+    V.wait_ge(S["vb"], 4)
+    V.tensor_tensor_scan(T.s3[:], T.r3[:], T.v3[:], 2 * LARGE, OP.add, OP.min).then_inc(S["s3"], 1)
+    make(2, T.o2, 2)
+    V.wait_ge(S["s3"], 1)
+    V.tensor_scalar(T.o3[:], T.s3[:, 128:516:129], 4.0, None, OP.mult).then_inc(S["o3"], 1)
+    make(2, T.o2, 3)
     V.wait_ge(S["o3"], 1)
-    V.wait_ge(S["g2"], 4)
     V.wait_ge(S["dq3"], 1)
-    make(3, T.o3)
+    V.wait_ge(S["g2"], 4)
+    make(3, T.o3, 0, 1, 2, 3)
     V.wait_ge(S["g3"], 4)
     V.quantize_mx(cdv, sdv, T.m[:, 0:768]).then_inc(S["qd"], 1)
     V.wait_ge(S["ldx"], 16)
-    V.quantize_mx(T.xq[:], T.xs[:], T.xb[:]).then_inc(S["qx"], 1)
+    for t in range(RD):
+        V.quantize_mx(T.xq[:, SH * t:SH * t + SH], T.xs[:, SH * t:SH * t + SH], T.xb[:, 512 * t:512 * t + 512]).then_inc(S["qx%d" % t], 1)
 
     def quarter(t):
         A.activation(T.dq[:, 256 * (t - 1):256 * t], T.dlb[:, 256 * (t - 1):256 * t], AF.Copy, scale=0.25).then_inc(S["dq%d" % t], 1)
@@ -208,13 +214,13 @@ def rank_program(g, core, T, topo):
     A.wait_ge(S["tb2"], 1)
     A.wait_ge(S["kk1"], 1)
     for s in range(4):
-        A.activation(T.v2[:, 65 * s:65 * s + CH], T.kk[:, 0:CH], AF.Abs, bias=T.bi[:, s:s + 1], scale=16384.0).then_inc(S["va%d" % s], 1)
+        A.activation(T.v2[:, 65 * s:65 * s + CH], T.kk[:, 0:CH], AF.Abs, bias=T.bi[:, s:s + 1], scale=4096.0).then_inc(S["va"], 1)
     quarter(2)
     A.wait_ge(S["kk2"], 1)
     A.wait_ge(S["bis"], 2)
     A.activation(T.vs[:], T.kk[:], AF.Abs, bias=T.bis[:], scale=4096.0).then_inc(S["vs"], 1)
     for s in range(4):
-        A.activation(T.v3[:, 129 * s:129 * s + 128], T.kk[:, 0:128], AF.Abs, bias=T.bi[:, 4 + s:5 + s], scale=16384.0).then_inc(S["vb%d" % s], 1)
+        A.activation(T.v3[:, 129 * s:129 * s + 128], T.kk[:, 0:128], AF.Abs, bias=T.bi[:, 4 + s:5 + s], scale=4096.0).then_inc(S["vb"], 1)
     quarter(3)
 
     def bank(k, n):
@@ -223,20 +229,21 @@ def rank_program(g, core, T, topo):
     def xt(t):
         return T.xq[:, SH * t:SH * t + SH], T.xs[:, SH * t:SH * t + SH]
 
-    PE.wait_ge(S["qx"], 1)
     PE.wait_ge(S["qb"], 1)
     for q in near_r + far_r:
         PE.wait_ge(S["base%d" % q], 2 * nb[q])
     for t in range(RD):
+        PE.wait_ge(S["qx%d" % t], 1)
         PE.matmul_mx(bank(t, 512), xt(t)[0], xt(t)[1], T.cb[:], T.sb[:], True, True).then_inc(S["pb%d" % t], 1)
     banks = {(1, mine): 4, (2, mine): 5, (3, mine): 6, (1, other): 7, (2, other): 0, (3, other): 1}
+    first = {1: 128, 2: 64, 3: 0}
 
     def changed(p):
         for t in (1, 2, 3):
             k = banks[(t, p)]
             if k < RD:
                 PE.wait_ge(S["cb%d" % k], 1 if k == 0 else 2)
-            lo, hi = 384 * p + CH * (3 - t), 384 * p + 384
+            lo, hi = 384 * p + first[t], 384 * p + 384
             PE.matmul_mx(bank(k, hi - lo), xt(t)[0], xt(t)[1], T.cd[:, lo:hi], T.sd[:, lo:hi], True, True).then_inc(S["pd%d%d" % (t, p)], 1)
 
     PE.wait_ge(S["qd"], 1)
@@ -263,52 +270,52 @@ def rank_program(g, core, T, topo):
 
     def changed_copy(q, cp, t, p):
         q.wait_ge(S["pd%d%d" % (t, p)], 1)
-        k, w = 512 * banks[(t, p)], T["w%d%d" % (t, p)]
-        if t == 3:
-            cp(w[:, 0:384], T.ps[:, k:k + 384]).then_inc(S["cd%d%d" % (t, p)], 1)
+        k, w, f = 512 * banks[(t, p)], T["w%d%d" % (t, p)], first[t]
+        if t > 1:
+            cp(w[:, f:384], T.ps[:, k:k + 384 - f]).then_inc(S["cd%d%d" % (t, p)], 1)
             return
-        n = CH * t
-        for h in (0, 192):
-            cp(w[:, h + 192 - n:h + 192], T.ps[:, k + h:k + h + n]).then_inc(S["cd%d%d" % (t, p)], 1)
+        for h in (f, f + 192):
+            cp(w[:, h:h + CH], T.ps[:, k + h - f:k + h - f + CH]).then_inc(S["cd%d%d" % (t, p)], 1)
 
     def order(t, p):
         for h in (0, 1):
             q = 2 * p + h
             k = 8 * (4 * (t - 1) + q)
-            V.tensor_copy(T.tabt[:, k:k + 8], T.tab[:, 3 * q + t - 1:96:12]).then_inc(S["tt%d%d" % (t, p)], 1)
+            V.tensor_scalar(T.tabt[:, k:k + 8], T.tab[:, 3 * q + t - 1:96:12], -float(first[t]), None, OP.add).then_inc(S["tt%d%d" % (t, p)], 1)
 
     def pick(q, cp, t, p, lo=0, hi=2):
         q.wait_ge(S["tt%d%d" % (t, p)], 2)
         q.wait_ge(S["cb%d" % t], 2)
-        q.wait_ge(S["cd%d%d" % (t, p)], 1 if t == 3 else 2)
+        q.wait_ge(S["cd%d%d" % (t, p)], 2 if t == 1 else 1)
         k, c = 8 * (4 * (t - 1) + 2 * p), 512 * t + 256 * p
-        cp(T.yb[:, c + SH * lo:c + SH * hi], T["w%d%d" % (t, p)][:].indirect(T.tabt[:, k + 8 * lo:k + 8 * hi])).then_inc(S["ga%d%d" % (t, p)], hi - lo)
+        cp(T.yb[:, c + SH * lo:c + SH * hi],
+           T["w%d%d" % (t, p)][:, first[t]:640].indirect(T.tabt[:, k + 8 * lo:k + 8 * hi])).then_inc(S["ga%d%d" % (t, p)], hi - lo)
 
     base_copy(A, acopy, 0)
     A.wait_ge(S["cb0"], 1)
     A.dma_start(T.y[:, 0:512], T.yb[:, 0:512]).then_inc(S["st"], 16)
-    base_copy(V, vcopy, 1)
     base_copy(A, acopy, 2)
-    base_copy(V, vcopy, 3)
     changed_copy(A, acopy, 1, mine)
     changed_copy(A, acopy, 2, mine)
-    changed_copy(V, vcopy, 3, mine)
-    V.wait_ge(S["rep"], 128)
-    order(1, mine)
-    order(2, mine)
-    order(3, mine)
     pick(A, acopy, 1, mine)
     pick(A, acopy, 2, mine)
+    changed_copy(A, acopy, 1, other)
+    pick(A, acopy, 1, other)
+    pick(A, acopy, 2, other, 1, 2)
+    pick(A, acopy, 3, other, 1, 2)
+    base_copy(V, vcopy, 1)
+    base_copy(V, vcopy, 3)
+    changed_copy(V, vcopy, 3, mine)
+    V.wait_ge(S["rep"], 128)
+    for t in (1, 2, 3):
+        order(t, mine)
     pick(V, vcopy, 3, mine)
     for t in (1, 2, 3):
         order(t, other)
-    changed_copy(A, acopy, 1, other)
     changed_copy(V, vcopy, 2, other)
-    pick(A, acopy, 1, other)
     changed_copy(V, vcopy, 3, other)
-    pick(A, acopy, 2, other)
+    pick(V, vcopy, 2, other, 0, 1)
     pick(V, vcopy, 3, other, 0, 1)
-    pick(A, acopy, 3, other, 1, 2)
 
     SY.wait_ge(S["own"], 1)
     SY.dma_start(T.lst[:, 3 * rank:3 * rank + 3], T.sown[:]).then_inc(S["ownd"], 16)

from concourse.bass import DstId, RemoteDMATransfer
from concourse.mybir import dt, AluOpType, AxisListType, ActivationFunctionType

SCRATCH = {
    "m": ("sbuf", [128, 1280], "bfloat16"),
    "dlb": ("sbuf", [128, 768], "bfloat16"),
    "dq": ("sbuf", [128, 768], "bfloat16"),
    "ltab": ("sbuf", [128, 12], "int32"),
    "lrow": ("sbuf", [1, 192], "int32"),
    "lb": ("sbuf", [128, 192], "int32"),
    "pc": ("sbuf", [128, 192], "float32"),
    "pcs": ("sbuf", [128, 192], "float32"),
    "kk": ("sbuf", [128, 192], "float32"),
    "v2": ("sbuf", [128, 260], "bfloat16"),
    "v3": ("sbuf", [128, 516], "bfloat16"),
    "r2": ("sbuf", [128, 260], "bfloat16"),
    "r3": ("sbuf", [128, 516], "bfloat16"),
    "s2": ("sbuf", [128, 260], "bfloat16"),
    "s3": ("sbuf", [128, 516], "bfloat16"),
    "vs": ("sbuf", [128, 192], "float32"),
    "vm": ("sbuf", [128, 192], "float32"),
    "bi": ("sbuf", [128, 8], "float32"),
    "o1": ("sbuf", [128, 4], "uint16"),
    "o2": ("sbuf", [128, 4], "uint16"),
    "o3": ("sbuf", [128, 4], "uint16"),
    "pi": ("sbuf", [128, 1], "int32"),
    "pa": ("sbuf", [128, 1], "int32"),
    "pb": ("sbuf", [128, 1], "int32"),
    "pf": ("sbuf", [128, 1], "float32"),
    "pj": ("sbuf", [128, 1], "float32"),
    "bis": ("sbuf", [128, 1], "float32"),
    "bas": ("sbuf", [128, 1], "float32"),
    "sown": ("sbuf", [128, 3], "uint16"),
    "lst": ("sbuf", [128, 12], "uint16"),
    "tab": ("sbuf", [128, 96], "uint16"),
    "tabt": ("sbuf", [128, 96], "uint16"),
    "cb": ("sbuf", [128, 512], "float8_e4m3fn_x4"),
    "sb": ("sbuf", [128, 512], "uint8"),
    "cd": ("sbuf", [128, 768], "float8_e4m3fn_x4"),
    "sd": ("sbuf", [128, 768], "uint8"),
    "xb": ("sbuf", [128, 2048], "bfloat16"),
    "xq": ("sbuf", [128, 512], "float8_e4m3fn_x4"),
    "xs": ("sbuf", [128, 512], "uint8"),
    "yb": ("sbuf", [128, 2048], "float32"),
    "ps": ("psum", [128, 4096], "float32"),
}
for _t in (1, 2, 3):
    for _p in (0, 1):
        SCRATCH["w%d%d" % (_t, _p)] = ("sbuf", [128, 640], "float32")

SEMAPHORES = (["%s%d" % (n, q) for n in ("base", "chg", "lst") for q in range(4)]
              + ["sent", "ldw", "ldt", "ldr1", "ldr", "ldd", "ldx", "iot", "bc1", "bc2", "fill", "rz", "rs", "pcs", "pab", "pf",
                 "pj", "bis", "tb1", "tb2", "ba", "dq1", "dq2", "dq3", "qb", "qd", "kk1", "kk2", "va", "vb", "s2", "o2",
                 "s3", "o3", "g1", "g2", "g3", "vs", "vm", "own", "ownd", "rep", "st"]
              + ["%s%d" % (n, t) for n in ("qx", "pb", "cb") for t in range(4)]
              + ["%s%d%d" % (n, t, p) for n in ("pd", "cd", "ga", "tt") for t in (1, 2, 3) for p in (0, 1)])

OP = AluOpType
AF = ActivationFunctionType
SH, CH, RD = 128, 64, 4
LARGE = 2.0 ** 20


def rank_program(g, core, T, topo):
    rank = T.rank_of(core)
    if rank is None:
        return
    S = T.sem
    V, A, PE, SY = g.vector, g.scalar, g.tensor, g.sync
    peers = [c for c in T.cores if c != core]
    near = [c for c in peers if c in topo.cores_of(core)]
    far = [c for c in peers if c not in topo.cores_of(core)]
    near_r = [T.rank_of(c) for c in near]
    far_r = [T.rank_of(c) for c in far]
    far_e = topo.engines(core, far[0])
    near_e = [e for e in topo.engines(core, near[0]) if e not in far_e][:len(far_e) * len(near) // len(far)]
    half = rank % 2
    mine, other = rank // 2, 1 - rank // 2

    def ids(cores):
        out = []
        for c in cores:
            rid, pid = topo.addr(c, core)
            out.append(DstId(rid=rid, pnc=pid))
        return out

    def bits(engs):
        return sum(1 << e for e in engs)

    def send(dst, src, sem):
        g.remote_dma_fused([
            RemoteDMATransfer(dst_ids=ids(far), dma_engine_mask=bits(far_e), remote_sem=S[sem], srcs=[src], dsts=[dst] * len(far)),
            RemoteDMATransfer(dst_ids=ids(near), dma_engine_mask=bits(near_e), remote_sem=S[sem], srcs=[src], dsts=[dst] * len(near)),
        ], local_sem=S["sent"])
        return len(far_e) + len(near_e)

    nb = {}
    for q in far_r:
        nb[q] = len(far_e)
    for q in near_r:
        nb[q] = len(near_e)
    cbv, sbv = T.cb[:, SH * rank:SH * rank + SH], T.sb[:, SH * rank:SH * rank + SH]
    cdv, sdv = T.cd[:, 192 * rank:192 * rank + 192], T.sd[:, 192 * rank:192 * rank + 192]

    def row(t):
        A.dma_start(T.lrow[0:1, CH * (t - 1):CH * t], T.idx[:, 4 * (t - 1):4 * t]).then_inc(S["ldr1" if t == 1 else "ldr"], 16)

    SY.dma_start(T.m[:, 768:1280], T.wm[:]).then_inc(S["ldw"], 16)
    row(1)
    A.dma_start(T.dlb[:], T.dl[:]).then_inc(S["ldd"], 16)
    row(2)
    row(3)
    for k in range(5):
        SY.dma_start(T.ltab[16 * k:16 * k + 16, :], T.idx[:]).then_inc(S["ldt"], 16)
    for k in range(5, 8):
        A.dma_start(T.ltab[16 * k:16 * k + 16, :], T.idx[:]).then_inc(S["ldt"], 16)
    SY.dma_start(T.xb[:], T.x[:]).then_inc(S["ldx"], 16)

    g.iota(T.pi[:], [[0, 1]], 0, 1).then_inc(S["iot"], 1)
    g.iota(T.pc[:], [[-CH, 3], [1, 16], [16, 4]], 128, 0, allow_small_or_imprecise_dtypes=True).then_inc(S["iot"], 1)
    g.wait_ge(S["ldr1"], 16)
    g.partition_broadcast(T.lb[:, 0:CH], T.lrow[0:1, 0:CH], 128).then_inc(S["bc1"], 1)
    g.wait_ge(S["ldr"], 32)
    g.partition_broadcast(T.lb[:, CH:192], T.lrow[0:1, CH:192], 128).then_inc(S["bc2"], 1)
    sent = 0
    g.wait_ge(S["qb"], 1)
    sent += send(cbv.bitcast(dt.uint8), cbv.bitcast(dt.uint8), "base%d" % rank)
    g.wait_ge(S["own"], 1)
    sent += send(T.lst[:, 3 * rank:3 * rank + 3], T.sown[:], "lst%d" % rank)
    sent += send(sbv, sbv, "base%d" % rank)
    g.wait_ge(S["qd"], 1)
    sent += send(cdv.bitcast(dt.uint8), cdv.bitcast(dt.uint8), "chg%d" % rank)
    sent += send(sdv, sdv, "chg%d" % rank)
    g.wait_ge(S["sent"], sent)

    V.memset(T.r2[:], 0.0).then_inc(S["rz"], 1)
    V.memset(T.r3[:], 0.0).then_inc(S["rz"], 1)
    V.memset(T.w10[:, 192:320], 0.0).then_inc(S["fill"], 1)
    V.memset(T.w11[:, 192:320], 0.0).then_inc(S["fill"], 1)
    V.wait_ge(S["iot"], 2)
    V.tensor_scalar(T.pcs[:], T.pc[:], 1.0 / 4096, None, OP.mult).then_inc(S["pcs"], 1)
    V.tensor_scalar(T.pa[:], T.pi[:], 7, None, OP.bitwise_and).then_inc(S["pab"], 1)
    V.tensor_scalar(T.pb[:], T.pi[:], 3, None, OP.logical_shift_right).then_inc(S["pab"], 1)
    V.wait_ge(S["rz"], 2)
    V.memset(T.r2[:, 0:260:65], LARGE).then_inc(S["rs"], 1)
    V.memset(T.r3[:, 0:516:129], LARGE).then_inc(S["rs"], 1)
    V.wait_ge(S["pab"], 2)
    V.tensor_scalar(T.pf[:], T.pa[:], 16.0, None, OP.mult).then_inc(S["pf"], 1)
    V.wait_ge(S["pf"], 1)
    V.tensor_tensor(T.pj[:], T.pf[:], T.pb[:], OP.add).then_inc(S["pj"], 1)
    V.wait_ge(S["pj"], 1)
    V.tensor_scalar(T.bis[:], T.pj[:], -4096.0, float(192 * half), OP.mult, OP.add).then_inc(S["bis"], 1)
    V.tensor_scalar(T.bas[:], T.pj[:], float(384 + SH * half), None, OP.add).then_inc(S["bis"], 1)
    V.wait_ge(S["bis"], 2)
    V.wait_ge(S["rs"], 2)
    V.wait_ge(S["fill"], 2)
    V.wait_ge(S["pcs"], 1)
    V.wait_ge(S["ldw"], 16)
    V.quantize_mx(cbv, sbv, T.m[:, 768:1280]).then_inc(S["qb"], 1)
    V.wait_ge(S["ldt"], 128)
    V.tensor_scalar(T.bi[:], T.ltab[:, 4:12], -4096.0, -64.0, OP.mult, OP.add).then_inc(S["tb2"], 1)
    V.tensor_scalar(T.o1[:], T.ltab[:, 0:4], 4.0, None, OP.mult).then_inc(S["tb1"], 1)
    V.tensor_scalar(T.v2[:, 64:260:65], T.ltab[:, 4:8], 128.0, None, OP.add).then_inc(S["ba"], 1)
    V.tensor_scalar(T.v3[:, 128:516:129], T.ltab[:, 8:12], 128.0, None, OP.add).then_inc(S["ba"], 1)
    V.wait_ge(S["bc1"], 1)
    V.tensor_tensor(T.kk[:, 0:CH], T.lb[:, 0:CH], T.pcs[:, 0:CH], OP.add).then_inc(S["kk1"], 1)

    def make(t, off, *es):
        lo = 256 * (RD - t)
        for e in es:
            V.tensor_tensor(T.m[:, lo - 256 + e:lo:4], T.m[:, lo + e:1280].indirect(off[:, 0:4]),
                            T.dq[:, 256 * (t - 1) + e:256 * t:4], OP.add).then_inc(S["g%d" % t], 1)

    V.wait_ge(S["tb1"], 1)
    V.wait_ge(S["dq1"], 1)
    make(1, T.o1, 0, 1, 2)
    V.wait_ge(S["bc2"], 1)
    V.tensor_tensor(T.kk[:, CH:192], T.lb[:, CH:192], T.pcs[:, CH:192], OP.add).then_inc(S["kk2"], 1)
    V.wait_ge(S["ba"], 2)
    V.wait_ge(S["va"], 4)
    V.tensor_tensor_scan(T.s2[:], T.r2[:], T.v2[:], 2 * LARGE, OP.add, OP.min).then_inc(S["s2"], 1)
    make(1, T.o1, 3)
    V.wait_ge(S["s2"], 1)
    V.tensor_scalar(T.o2[:], T.s2[:, 64:260:65], 4.0, -256.0, OP.mult, OP.add).then_inc(S["o2"], 1)
    V.wait_ge(S["vs"], 1)
    V.tensor_tensor_scan(T.vm[:], T.vs[:], T.vs[:], 1.0e9, OP.min, OP.min).then_inc(S["vm"], 1)
    V.wait_ge(S["o2"], 1)
    V.wait_ge(S["g1"], 4)
    V.wait_ge(S["dq2"], 1)
    V.wait_ge(S["vm"], 1)
    V.tensor_scalar(T.sown[:], T.vm[:, CH - 1:192:CH], T.bas[:], None, OP.min).then_inc(S["own"], 1)
    make(2, T.o2, 0, 1)
    V.wait_ge(S["vb"], 4)
    V.tensor_tensor_scan(T.s3[:], T.r3[:], T.v3[:], 2 * LARGE, OP.add, OP.min).then_inc(S["s3"], 1)
    make(2, T.o2, 2)
    V.wait_ge(S["s3"], 1)
    V.tensor_scalar(T.o3[:], T.s3[:, 128:516:129], 4.0, None, OP.mult).then_inc(S["o3"], 1)
    make(2, T.o2, 3)
    V.wait_ge(S["o3"], 1)
    V.wait_ge(S["dq3"], 1)
    V.wait_ge(S["g2"], 4)
    make(3, T.o3, 0, 1, 2, 3)
    V.wait_ge(S["g3"], 4)
    V.quantize_mx(cdv, sdv, T.m[:, 0:768]).then_inc(S["qd"], 1)
    V.wait_ge(S["ldx"], 16)
    for t in range(RD):
        V.quantize_mx(T.xq[:, SH * t:SH * t + SH], T.xs[:, SH * t:SH * t + SH], T.xb[:, 512 * t:512 * t + 512]).then_inc(S["qx%d" % t], 1)

    def quarter(t):
        A.activation(T.dq[:, 256 * (t - 1):256 * t], T.dlb[:, 256 * (t - 1):256 * t], AF.Copy, scale=0.25).then_inc(S["dq%d" % t], 1)

    A.wait_ge(S["ldd"], 16)
    quarter(1)
    A.wait_ge(S["tb2"], 1)
    A.wait_ge(S["kk1"], 1)
    for s in range(4):
        A.activation(T.v2[:, 65 * s:65 * s + CH], T.kk[:, 0:CH], AF.Abs, bias=T.bi[:, s:s + 1], scale=4096.0).then_inc(S["va"], 1)
    quarter(2)
    A.wait_ge(S["kk2"], 1)
    A.wait_ge(S["bis"], 2)
    A.activation(T.vs[:], T.kk[:], AF.Abs, bias=T.bis[:], scale=4096.0).then_inc(S["vs"], 1)
    for s in range(4):
        A.activation(T.v3[:, 129 * s:129 * s + 128], T.kk[:, 0:128], AF.Abs, bias=T.bi[:, 4 + s:5 + s], scale=4096.0).then_inc(S["vb"], 1)
    quarter(3)

    def bank(k, n):
        return T.ps[:, 512 * k:512 * k + n]

    def xt(t):
        return T.xq[:, SH * t:SH * t + SH], T.xs[:, SH * t:SH * t + SH]

    PE.wait_ge(S["qb"], 1)
    for q in near_r + far_r:
        PE.wait_ge(S["base%d" % q], 2 * nb[q])
    for t in range(RD):
        PE.wait_ge(S["qx%d" % t], 1)
        PE.matmul_mx(bank(t, 512), xt(t)[0], xt(t)[1], T.cb[:], T.sb[:], True, True).then_inc(S["pb%d" % t], 1)
    banks = {(1, mine): 4, (2, mine): 5, (3, mine): 6, (1, other): 7, (2, other): 0, (3, other): 1}
    first = {1: 128, 2: 64, 3: 0}

    def changed(p):
        for t in (1, 2, 3):
            k = banks[(t, p)]
            if k < RD:
                PE.wait_ge(S["cb%d" % k], 1 if k == 0 else 2)
            lo, hi = 384 * p + first[t], 384 * p + 384
            PE.matmul_mx(bank(k, hi - lo), xt(t)[0], xt(t)[1], T.cd[:, lo:hi], T.sd[:, lo:hi], True, True).then_inc(S["pd%d%d" % (t, p)], 1)

    PE.wait_ge(S["qd"], 1)
    for q in near_r:
        PE.wait_ge(S["chg%d" % q], 2 * nb[q])
    changed(mine)
    for q in far_r:
        PE.wait_ge(S["chg%d" % q], 2 * nb[q])
    changed(other)

    def vcopy(out, in_):
        return V.tensor_copy(out, in_)

    def acopy(out, in_):
        return A.activation(out, in_, AF.Copy)

    def base_copy(q, cp, t):
        q.wait_ge(S["pb%d" % t], 1)
        if t == 0:
            cp(T.yb[:, 0:512], bank(0, 512)).then_inc(S["cb0"], 1)
            return
        for p in (0, 1):
            cp(T["w%d%d" % (t, p)][:, 384:640], T.ps[:, 512 * t + 256 * p:512 * t + 256 * p + 256]).then_inc(S["cb%d" % t], 1)

    def changed_copy(q, cp, t, p):
        q.wait_ge(S["pd%d%d" % (t, p)], 1)
        k, w, f = 512 * banks[(t, p)], T["w%d%d" % (t, p)], first[t]
        if t > 1:
            cp(w[:, f:384], T.ps[:, k:k + 384 - f]).then_inc(S["cd%d%d" % (t, p)], 1)
            return
        for h in (f, f + 192):
            cp(w[:, h:h + CH], T.ps[:, k + h - f:k + h - f + CH]).then_inc(S["cd%d%d" % (t, p)], 1)

    def order(t, p):
        for h in (0, 1):
            q = 2 * p + h
            k = 8 * (4 * (t - 1) + q)
            V.tensor_scalar(T.tabt[:, k:k + 8], T.tab[:, 3 * q + t - 1:96:12], -float(first[t]), None, OP.add).then_inc(S["tt%d%d" % (t, p)], 1)

    def pick(q, cp, t, p, lo=0, hi=2):
        q.wait_ge(S["tt%d%d" % (t, p)], 2)
        q.wait_ge(S["cb%d" % t], 2)
        q.wait_ge(S["cd%d%d" % (t, p)], 2 if t == 1 else 1)
        k, c = 8 * (4 * (t - 1) + 2 * p), 512 * t + 256 * p
        cp(T.yb[:, c + SH * lo:c + SH * hi],
           T["w%d%d" % (t, p)][:, first[t]:640].indirect(T.tabt[:, k + 8 * lo:k + 8 * hi])).then_inc(S["ga%d%d" % (t, p)], hi - lo)

    base_copy(A, acopy, 0)
    A.wait_ge(S["cb0"], 1)
    A.dma_start(T.y[:, 0:512], T.yb[:, 0:512]).then_inc(S["st"], 16)
    base_copy(A, acopy, 2)
    changed_copy(A, acopy, 1, mine)
    changed_copy(A, acopy, 2, mine)
    pick(A, acopy, 1, mine)
    pick(A, acopy, 2, mine)
    changed_copy(A, acopy, 1, other)
    pick(A, acopy, 1, other)
    pick(A, acopy, 2, other, 1, 2)
    pick(A, acopy, 3, other, 1, 2)
    base_copy(V, vcopy, 1)
    base_copy(V, vcopy, 3)
    changed_copy(V, vcopy, 3, mine)
    V.wait_ge(S["rep"], 128)
    for t in (1, 2, 3):
        order(t, mine)
    pick(V, vcopy, 3, mine)
    for t in (1, 2, 3):
        order(t, other)
    changed_copy(V, vcopy, 2, other)
    changed_copy(V, vcopy, 3, other)
    pick(V, vcopy, 2, other, 0, 1)
    pick(V, vcopy, 3, other, 0, 1)

    SY.wait_ge(S["own"], 1)
    SY.dma_start(T.lst[:, 3 * rank:3 * rank + 3], T.sown[:]).then_inc(S["ownd"], 16)
    SY.wait_ge(S["ownd"], 16)
    for q in near_r + far_r:
        SY.wait_ge(S["lst%d" % q], nb[q])
    for k in range(8):
        SY.dma_start(T.tab[16 * k:16 * k + 16, :], T.lst[:]).then_inc(S["rep"], 16)
    for p, turn in ((mine, (1, 3, 2)), (other, (1, 2, 3))):
        for t in turn:
            SY.wait_ge(S["ga%d%d" % (t, p)], 2)
            c = 512 * t + 256 * p
            SY.dma_start(T.y[:, c:c + 256], T.yb[:, c:c + 256]).then_inc(S["st"], 16)
    SY.wait_ge(S["st"], 16 * 7)
